import numpy as np, ml_dtypes
CORES = [17,81,89,18,82,90]
N = 6
import mx_ref
NC = 128
BF = ml_dtypes.bfloat16
def cut(t, i, w=512):
    return t[:, w * i:w * i + w]
def term(a, B):
    return np.stack([mx_ref.matmul(mx_ref.quantize(cut(a, i)), B) for i in range(4)], axis=2).reshape(128, -1)
def setup_inputs(rng):
    def f(*shape):
        return mx_ref.flush((rng.standard_normal(shape, dtype=np.float32) * np.exp2(rng.integers(-2, 3, shape[:-1] + (1,)))).astype(BF))
    return {"a": f(N, 128, 4 * 512), "b": f(N, 128, 2 * 4 * NC)}
def setup_inputs_blocks(rng):
    d = setup_inputs(rng)
    for k in ("a", "b"): d[k] = mx_ref.spread(d[k], rng, 2)
    return d
def setup_inputs_wide(rng):
    d = setup_inputs(rng)
    for k in ("a", "b"): d[k] = mx_ref.flush((d[k].astype(np.float32) * np.exp2(rng.integers(-4, 5, (N, 1, 1))).astype(np.float32)).astype(BF))
    return d
def setup_inputs_lossless(rng):
    a = np.zeros((N, 128, 4 * 128, 4), np.float32)
    for r in range(N):
        k = rng.integers(0, 512, size=4 * 128)
        a[r, k // 4, np.arange(4 * 128), k % 4] = 1.0
    size = np.tile(np.repeat(2.0 ** rng.integers(-4, 5, size=(1, 1, NC)), 4, axis=2), (1, 1, 2))
    b = rng.integers(-1, 2, size=(N, 128, 2 * 4 * NC)) * size
    return {"a": a.reshape(N, 128, 4 * 512).astype(BF), "b": b.astype(np.float32).astype(BF)}
def reference(a, b):
    T = [term(a[r], mx_ref.quantize(cut(b[r], k, 4 * NC))) for r in range(N) for k in range(2)]
    y = np.zeros((N, 128, 4 * NC), np.float32)
    for c in range(N):
        y[c] = mx_ref.total(T[:2 * c + 2])
    return {"y": y}

@@ -1,0 +1,206 @@
+from concourse.bass import DstId, RemoteDMATransfer
+from concourse.mybir import dt, AluOpType, ActivationFunctionType
+
+SCRATCH = {
+    "at": ("sbuf", [128, 2048], "bfloat16"),
+    "bt": ("sbuf", [128, 1024], "bfloat16"),
+    "qa": ("sbuf", [128, 512], "float8_e4m3fn_x4"),
+    "sa": ("sbuf", [128, 512], "uint8"),
+    "qb": ("sbuf", [128, 256], "float8_e4m3fn_x4"),
+    "sb": ("sbuf", [128, 256], "uint8"),
+    "ones": ("sbuf", [128, 128], "bfloat16"),
+    "sel": ("sbuf", [128, 2048], "bfloat16"),
+    "qsel": ("sbuf", [128, 512], "float8_e4m3fn_x4"),
+    "ssel": ("sbuf", [128, 512], "uint8"),
+    "hp": ("sbuf", [128, 512], "bfloat16"),
+    "qp": ("sbuf", [128, 128], "float8_e4m3fn_x4"),
+    "sp": ("sbuf", [128, 128], "uint8"),
+    "hs": ("sbuf", [128, 512], "bfloat16"),
+    "qs": ("sbuf", [128, 128], "float8_e4m3fn_x4"),
+    "ss": ("sbuf", [128, 128], "uint8"),
+    "yt": ("sbuf", [128, 512], "float32"),
+    "ps": ("psum", [128, 4096], "float32"),
+}
+SLOTS = 3
+for _k in range(SLOTS):
+    SCRATCH["ql%d" % _k] = ("sbuf", [128, 128], "float8_e4m3fn_x4")
+    SCRATCH["sl%d" % _k] = ("sbuf", [128, 128], "uint8")
+SEMAPHORES = ["ldb", "lda0", "lda1", "v", "s", "t", "gs", "sent", "st"] + ["arr%d" % _k for _k in range(SLOTS)]
+
+
+def make_plan(cores, topo):
+    n = len(cores)
+    pairs = [(l, h) for l in range(n) for h in range(l + 1, n) if topo.chip(cores[l]) == topo.chip(cores[h])]
+    msgs = []
+    for l, h in pairs:
+        msgs.append((l, h, "P", (l, h)))
+        for d in range(n):
+            if d in (l, h) or d < l:
+                continue
+            direct = topo.may_write(cores[l], cores[d])
+            if d > h:
+                msgs.append((l if direct else h, d, "S", (l, h)))
+            else:
+                msgs.append((l, d, "P", (l, h)) if direct else (h, d, "F", (l, h)))
+        if any(m[0] == l and m[2] == "S" for m in msgs):
+            msgs.append((h, l, "P", (l, h)))
+
+    def hops(m):
+        a, b = topo.chip(cores[m[0]]), topo.chip(cores[m[1]])
+        return 0 if a == b else 1 if topo.mates(a, b) or topo.same_plane(a, b) else 2
+
+    def due(m):
+        return hops(m) > 0, "PFS".index(m[2]), hops(m)
+
+    slot = {}
+    for d in range(n):
+        mine = sorted([m for m in msgs if m[1] == d], key=due)
+        mine.sort(key=lambda m: m[2] == "F" and len([f for f in msgs if f[0] == m[0] and f[2] == "F"]) > 1)
+        for k, m in enumerate(mine):
+            slot[m] = k
+    return msgs, slot, hops, due
+
+
+def rank_program(g, core, T, topo):
+    rank = T.rank_of(core)
+    if rank is None:
+        return
+    cores = T.cores
+    msgs, slot, hops, due = make_plan(cores, topo)
+    inbox = sorted([m for m in msgs if m[1] == rank], key=due)
+    outbox = [m for m in msgs if m[0] == rank]
+    pair = [m[3] for m in msgs if rank in m[3]][0]
+    from_partner = [m for m in inbox if m[0] in pair]
+    addends = [m for m in inbox if m[0] not in pair or rank == pair[1]]
+    forwards = sorted([m for m in outbox if m[2] == "F"], key=hops, reverse=True)
+    sends_p = any(m[2] == "P" for m in outbox)
+    sends_s = any(m[2] == "S" for m in outbox)
+
+    queue = {"g": g, "v": g.vector, "s": g.scalar, "t": g.tensor, "y": g.sync}
+    count = {k: 0 for k in SEMAPHORES}
+    seen = {}
+
+    def need(q, sem, n):
+        if n and seen.get((q, sem), 0) < n:
+            queue[q].wait_ge(T.sem[sem], n)
+            seen[(q, sem)] = n
+
+    def did(sem, call, n=1):
+        call.then_inc(T.sem[sem], n)
+        count[sem] += n
+        return count[sem]
+
+    def words(name, k=0):
+        return T[name][:, 128 * k:128 * k + 128]
+
+    def arrivals(m):
+        return 2 * bin(topo.mask(cores[m[0]], cores[m[1]])).count("1")
+
+    did("ldb", g.sync.dma_start(T.bt[:, :], T.b[:, :]), 16)
+    did("lda0", g.sync.dma_start(T.at[:, 0:1024], T.a[:, 0:1024]), 16)
+    did("lda1", g.sync.dma_start(T.at[:, 1024:2048], T.a[:, 1024:2048]), 16)
+
+    did("v", g.vector.memset(T.ones[:, :], 1.0))
+    filled = did("v", g.vector.memset(T.sel[:, :], 0.0))
+    need("g", "v", filled)
+    for b in range(4):
+        made = did("gs", g.affine_select(T.sel[:, 512 * b + b:512 * b + 512:4], T.ones[:, :], [[-1, 128]],
+                                         AluOpType.is_equal, 0.0, 0, 1))
+
+    need("v", "ldb", 16)
+    did("v", g.vector.quantize_mx(T.qb[:, :], T.sb[:, :], T.bt[:, :]))
+    ready = []
+    for i in range(4):
+        need("v", "lda%d" % (i // 2), 16)
+        ready.append(did("v", g.vector.quantize_mx(words("qa", i), words("sa", i), T.at[:, 512 * i:512 * i + 512])))
+
+    bank = [0] * 4
+    state = {"set": 1, "readers": [{}, {}]}
+
+    def region(i):
+        c = 2048 * state["set"] + 512 * i
+        return T.ps[:, c:c + 128]
+
+    def build(tiles):
+        state["set"] = 1 - state["set"]
+        readers = state["readers"][state["set"]]
+        for q in readers:
+            need("t", q, readers[q])
+        for i in range(4):
+            need("t", "v", ready[i])
+            for k in range(2):
+                call = g.tensor.matmul_mx(region(i), words("qa", i), words("sa", i), words("qb", k), words("sb", k),
+                                          k == 0, k == 1 and not tiles)
+            bank[i] = did("t", call)
+        for m in tiles:
+            k = slot[m]
+            need("t", "v", selected[0])
+            need("t", "arr%d" % k, arrivals(m))
+            for b in range(4):
+                bank[b] = did("t", g.tensor.matmul_mx(region(b), words("qsel", b), words("ssel", b), T["ql%d" % k][:, :],
+                                                      T["sl%d" % k][:, :], False, m == tiles[-1]))
+
+    def copy_out(name, by):
+        last = state["readers"][state["set"]]
+        for i in range(4):
+            q = by[i]
+            need(q, "t", bank[i])
+            view = T[name][:, i:512:4]
+            if q == "s":
+                last[q] = did(q, g.scalar.activation(view, region(i), ActivationFunctionType.Copy))
+            else:
+                last[q] = did(q, g.vector.tensor_copy(view, region(i)))
+        return last
+
+    def pack(name, codes, plane, by):
+        last = copy_out(name, by)
+        for q in last:
+            need("v", q, last[q])
+        packed = did("v", g.vector.quantize_mx(T[codes][:, :], T[plane][:, :], T[name][:, :]))
+        need("g", "v", packed)
+
+    def store(by):
+        last = copy_out("yt", by)
+        for q in last:
+            need("y", q, last[q])
+        did("st", g.sync.dma_start(T.y[:, :], T.yt[:, :]), 16)
+
+    def send(group, codes, plane):
+        engines = topo.mask(cores[rank], cores[group[0][1]])
+        sem = T.sem["arr%d" % slot[group[0]]]
+        ids = [DstId(rid=topo.addr(cores[m[1]])[0], pnc=topo.addr(cores[m[1]])[1]) for m in group]
+        for src, dsts in ((T[codes][:, :].bitcast(dt.uint8), [T["ql%d" % slot[m]][:, :].bitcast(dt.uint8) for m in group]),
+                          (T[plane][:, :], [T["sl%d" % slot[m]][:, :] for m in group])):
+            g.remote_dma_fused([RemoteDMATransfer(dst_ids=ids, dma_engine_mask=engines, remote_sem=sem, srcs=[src], dsts=dsts)],
+                               local_sem=T.sem.sent)
+            count["sent"] += bin(engines).count("1")
+
+    P_BY, Y_BY = "sssv", "svsv"
+    if sends_p or not addends:
+        build([])
+        if sends_p:
+            pack("hp", "qp", "sp", P_BY)
+            for m in sorted([m for m in outbox if m[2] == "P"], key=hops):
+                send([m], "qp", "sp")
+        if not addends:
+            store(P_BY)
+    need("v", "gs", made)
+    selected = [did("v", g.vector.quantize_mx(T.qsel[:, :], T.ssel[:, :], T.sel[:, :]))]
+
+    if forwards:
+        k = slot[from_partner[0]]
+        need("g", "arr%d" % k, arrivals(from_partner[0]))
+        send(forwards, "ql%d" % k, "sl%d" % k)
+    if sends_s:
+        build(from_partner)
+        pack("hs", "qs", "ss", Y_BY)
+        for m in [m for m in outbox if m[2] == "S"]:
+            send([m], "qs", "ss")
+
+    if addends:
+        build(addends)
+        store(Y_BY)
+
+    for sem in ("v", "s", "t", "gs", "st"):
+        need("y", sem, count[sem])
+    need("g", "sent", count["sent"])

@@ -9,6 +9,7 @@ SCRATCH = {
     "qb": ("sbuf", [128, 256], "float8_e4m3fn_x4"),
     "sb": ("sbuf", [128, 256], "uint8"),
     "ones": ("sbuf", [128, 128], "bfloat16"),
+    "diag": ("sbuf", [128, 128], "bfloat16"),
     "sel": ("sbuf", [128, 2048], "bfloat16"),
     "qsel": ("sbuf", [128, 512], "float8_e4m3fn_x4"),
     "ssel": ("sbuf", [128, 512], "uint8"),
@@ -25,7 +26,8 @@ SLOTS = 3
 for _k in range(SLOTS):
     SCRATCH["ql%d" % _k] = ("sbuf", [128, 128], "float8_e4m3fn_x4")
     SCRATCH["sl%d" % _k] = ("sbuf", [128, 128], "uint8")
-SEMAPHORES = ["ldb", "lda0", "lda1", "v", "s", "t", "gs", "sent", "st"] + ["arr%d" % _k for _k in range(SLOTS)]
+SEMAPHORES = ["ldb", "lda0", "lda1", "v", "s", "t", "gs", "sent", "st", "arrsel"] + ["arr%d" % _k for _k in range(SLOTS)]
+SHARE = 32
 
 
 def make_plan(cores, topo):
@@ -70,8 +72,10 @@ def rank_program(g, core, T, topo):
     inbox = sorted([m for m in msgs if m[1] == rank], key=due)
     outbox = [m for m in msgs if m[0] == rank]
     pair = [m[3] for m in msgs if rank in m[3]][0]
-    from_partner = [m for m in inbox if m[0] in pair]
-    addends = [m for m in inbox if m[0] not in pair or rank == pair[1]]
+    lower = rank == pair[0]
+    partner = pair[1] if lower else pair[0]
+    from_partner = [m for m in inbox if m[0] == partner]
+    addends = [m for m in inbox if m[0] != partner or not lower]
     forwards = sorted([m for m in outbox if m[2] == "F"], key=hops, reverse=True)
     sends_p = any(m[2] == "P" for m in outbox)
     sends_s = any(m[2] == "S" for m in outbox)
@@ -93,19 +97,45 @@ def rank_program(g, core, T, topo):
     def words(name, k=0):
         return T[name][:, 128 * k:128 * k + 128]
 
-    def arrivals(m):
-        return 2 * bin(topo.mask(cores[m[0]], cores[m[1]])).count("1")
+    def engines(a, b):
+        return topo.mask(cores[a], cores[b])
+
+    def arrivals(a, b):
+        return 2 * bin(engines(a, b)).count("1")
+
+    def send(dsts, sem, codes, plane):
+        ids = [DstId(rid=topo.addr(cores[d[0]])[0], pnc=topo.addr(cores[d[0]])[1]) for d in dsts]
+        mask = engines(rank, dsts[0][0])
+        for src, lands in ((codes.bitcast(dt.uint8), [d[1].bitcast(dt.uint8) for d in dsts]), (plane, [d[2] for d in dsts])):
+            g.remote_dma_fused([RemoteDMATransfer(dst_ids=ids, dma_engine_mask=mask, remote_sem=T.sem[sem], srcs=[src], dsts=lands)],
+                               local_sem=T.sem.sent)
+            count["sent"] += bin(mask).count("1")
 
     did("ldb", g.sync.dma_start(T.bt[:, :], T.b[:, :]), 16)
     did("lda0", g.sync.dma_start(T.at[:, 0:1024], T.a[:, 0:1024]), 16)
     did("lda1", g.sync.dma_start(T.at[:, 1024:2048], T.a[:, 1024:2048]), 16)
 
-    did("v", g.vector.memset(T.ones[:, :], 1.0))
-    filled = did("v", g.vector.memset(T.sel[:, :], 0.0))
-    need("g", "v", filled)
-    for b in range(4):
-        made = did("gs", g.affine_select(T.sel[:, 512 * b + b:512 * b + 512:4], T.ones[:, :], [[-1, 128]],
-                                         AluOpType.is_equal, 0.0, 0, 1))
+    lo, hi = (0, 512 - SHARE) if lower else (SHARE, 512)
+    first = 0 if lower else 3
+    mine, theirs = ((0, SHARE), (512 - SHARE, 512)) if lower else ((512 - SHARE, 512), (0, SHARE))
+    rest = (128, hi) if lower else (lo, 384)
+    ones = did("v", g.vector.memset(T.ones[:, :], 1.0))
+    zero = [did("v", g.vector.memset(T.sel[:, 512 * first:512 * first + 512], 0.0))]
+    zero.append(did("v", g.vector.memset(T.sel[:, 4 * rest[0]:4 * rest[1]], 0.0)))
+    need("g", "v", ones)
+    made = did("gs", g.affine_select(T.diag[:, :], T.ones[:, :], [[-1, 128]], AluOpType.is_equal, 0.0, 0, 1))
+    need("s", "gs", made)
+    placed = []
+    for b in [first] + [b for b in range(4) if b != first]:
+        need("s", "v", zero[b != first])
+        a, z = max(lo, 128 * b), min(hi, 128 * b + 128)
+        placed.append(did("s", g.scalar.activation(T.sel[:, 4 * a + b:4 * z:4], T.diag[:, a - 128 * b:z - 128 * b],
+                                                   ActivationFunctionType.Copy)))
+    need("v", "s", placed[0])
+    share = did("v", g.vector.quantize_mx(words("qsel", first), words("ssel", first), T.sel[:, 512 * first:512 * first + 512]))
+    need("g", "v", share)
+    codes, plane = T.qsel[:, mine[0]:mine[1]], T.ssel[:, mine[0]:mine[1]]
+    send([(partner, codes, plane)], "arrsel", codes, plane)
 
     need("v", "ldb", 16)
     did("v", g.vector.quantize_mx(T.qb[:, :], T.sb[:, :], T.bt[:, :]))
@@ -135,7 +165,8 @@ def rank_program(g, core, T, topo):
         for m in tiles:
             k = slot[m]
             need("t", "v", selected[0])
-            need("t", "arr%d" % k, arrivals(m))
+            need("t", "arrsel", arrivals(partner, rank))
+            need("t", "arr%d" % k, arrivals(m[0], rank))
             for b in range(4):
                 bank[b] = did("t", g.tensor.matmul_mx(region(b), words("qsel", b), words("ssel", b), T["ql%d" % k][:, :],
                                                       T["sl%d" % k][:, :], False, m == tiles[-1]))
@@ -165,15 +196,9 @@ def rank_program(g, core, T, topo):
             need("y", q, last[q])
         did("st", g.sync.dma_start(T.y[:, :], T.yt[:, :]), 16)
 
-    def send(group, codes, plane):
-        engines = topo.mask(cores[rank], cores[group[0][1]])
-        sem = T.sem["arr%d" % slot[group[0]]]
-        ids = [DstId(rid=topo.addr(cores[m[1]])[0], pnc=topo.addr(cores[m[1]])[1]) for m in group]
-        for src, dsts in ((T[codes][:, :].bitcast(dt.uint8), [T["ql%d" % slot[m]][:, :].bitcast(dt.uint8) for m in group]),
-                          (T[plane][:, :], [T["sl%d" % slot[m]][:, :] for m in group])):
-            g.remote_dma_fused([RemoteDMATransfer(dst_ids=ids, dma_engine_mask=engines, remote_sem=sem, srcs=[src], dsts=dsts)],
-                               local_sem=T.sem.sent)
-            count["sent"] += bin(engines).count("1")
+    def post(group, codes, plane):
+        send([(m[1], T["ql%d" % slot[m]][:, :], T["sl%d" % slot[m]][:, :]) for m in group], "arr%d" % slot[group[0]],
+             T[codes][:, :], T[plane][:, :])
 
     P_BY, Y_BY = "sssv", "svsv"
     if sends_p or not addends:
@@ -181,21 +206,22 @@ def rank_program(g, core, T, topo):
         if sends_p:
             pack("hp", "qp", "sp", P_BY)
             for m in sorted([m for m in outbox if m[2] == "P"], key=hops):
-                send([m], "qp", "sp")
+                post([m], "qp", "sp")
         if not addends:
             store(P_BY)
-    need("v", "gs", made)
-    selected = [did("v", g.vector.quantize_mx(T.qsel[:, :], T.ssel[:, :], T.sel[:, :]))]
+    need("v", "s", placed[-1])
+    selected = [did("v", g.vector.quantize_mx(T.qsel[:, rest[0]:rest[1]], T.ssel[:, rest[0]:rest[1]],
+                                              T.sel[:, 4 * rest[0]:4 * rest[1]]))]
 
     if forwards:
         k = slot[from_partner[0]]
-        need("g", "arr%d" % k, arrivals(from_partner[0]))
-        send(forwards, "ql%d" % k, "sl%d" % k)
+        need("g", "arr%d" % k, arrivals(partner, rank))
+        post(forwards, "ql%d" % k, "sl%d" % k)
     if sends_s:
         build(from_partner)
         pack("hs", "qs", "ss", Y_BY)
         for m in [m for m in outbox if m[2] == "S"]:
-            send([m], "qs", "ss")
+            post([m], "qs", "ss")
 
     if addends:
         build(addends)

from concourse.bass import DstId, RemoteDMATransfer
from concourse.mybir import dt, AluOpType, ActivationFunctionType

SCRATCH = {
    "at": ("sbuf", [128, 2048], "bfloat16"),
    "bt": ("sbuf", [128, 1024], "bfloat16"),
    "qa": ("sbuf", [128, 512], "float8_e4m3fn_x4"),
    "sa": ("sbuf", [128, 512], "uint8"),
    "qb": ("sbuf", [128, 256], "float8_e4m3fn_x4"),
    "sb": ("sbuf", [128, 256], "uint8"),
    "ones": ("sbuf", [128, 128], "bfloat16"),
    "diag": ("sbuf", [128, 128], "bfloat16"),
    "sel": ("sbuf", [128, 2048], "bfloat16"),
    "qsel": ("sbuf", [128, 512], "float8_e4m3fn_x4"),
    "ssel": ("sbuf", [128, 512], "uint8"),
    "hp": ("sbuf", [128, 512], "bfloat16"),
    "qp": ("sbuf", [128, 128], "float8_e4m3fn_x4"),
    "sp": ("sbuf", [128, 128], "uint8"),
    "hs": ("sbuf", [128, 512], "bfloat16"),
    "qs": ("sbuf", [128, 128], "float8_e4m3fn_x4"),
    "ss": ("sbuf", [128, 128], "uint8"),
    "yt": ("sbuf", [128, 512], "float32"),
    "ps": ("psum", [128, 4096], "float32"),
}
SLOTS = 3
for _k in range(SLOTS):
    SCRATCH["ql%d" % _k] = ("sbuf", [128, 128], "float8_e4m3fn_x4")
    SCRATCH["sl%d" % _k] = ("sbuf", [128, 128], "uint8")
SEMAPHORES = ["ldb", "lda0", "lda1", "v", "s", "t", "gs", "sent", "st", "arrsel"] + ["arr%d" % _k for _k in range(SLOTS)]
SHARE = 32


def make_plan(cores, topo):
    n = len(cores)
    pairs = [(l, h) for l in range(n) for h in range(l + 1, n) if topo.chip(cores[l]) == topo.chip(cores[h])]
    msgs = []
    for l, h in pairs:
        msgs.append((l, h, "P", (l, h)))
        for d in range(n):
            if d in (l, h) or d < l:
                continue
            direct = topo.may_write(cores[l], cores[d])
            if d > h:
                msgs.append((l if direct else h, d, "S", (l, h)))
            else:
                msgs.append((l, d, "P", (l, h)) if direct else (h, d, "F", (l, h)))
        if any(m[0] == l and m[2] == "S" for m in msgs):
            msgs.append((h, l, "P", (l, h)))

    def hops(m):
        a, b = topo.chip(cores[m[0]]), topo.chip(cores[m[1]])
        return 0 if a == b else 1 if topo.mates(a, b) or topo.same_plane(a, b) else 2

    def due(m):
        return hops(m) > 0, "PFS".index(m[2]), hops(m)

    slot = {}
    for d in range(n):
        mine = sorted([m for m in msgs if m[1] == d], key=due)
        mine.sort(key=lambda m: m[2] == "F" and len([f for f in msgs if f[0] == m[0] and f[2] == "F"]) > 1)
        for k, m in enumerate(mine):
            slot[m] = k
    return msgs, slot, hops, due


def rank_program(g, core, T, topo):
    rank = T.rank_of(core)
    if rank is None:
        return
    cores = T.cores
    msgs, slot, hops, due = make_plan(cores, topo)
    inbox = sorted([m for m in msgs if m[1] == rank], key=due)
    outbox = [m for m in msgs if m[0] == rank]
    pair = [m[3] for m in msgs if rank in m[3]][0]
    lower = rank == pair[0]
    partner = pair[1] if lower else pair[0]
    from_partner = [m for m in inbox if m[0] == partner]
    addends = [m for m in inbox if m[0] != partner or not lower]
    forwards = sorted([m for m in outbox if m[2] == "F"], key=hops, reverse=True)
    sends_p = any(m[2] == "P" for m in outbox)
    sends_s = any(m[2] == "S" for m in outbox)

    queue = {"g": g, "v": g.vector, "s": g.scalar, "t": g.tensor, "y": g.sync}
    count = {k: 0 for k in SEMAPHORES}
    seen = {}

    def need(q, sem, n):
        if n and seen.get((q, sem), 0) < n:
            queue[q].wait_ge(T.sem[sem], n)
            seen[(q, sem)] = n

    def did(sem, call, n=1):
        call.then_inc(T.sem[sem], n)
        count[sem] += n
        return count[sem]

    def words(name, k=0):
        return T[name][:, 128 * k:128 * k + 128]

    def engines(a, b):
        return topo.mask(cores[a], cores[b])

    def arrivals(a, b):
        return 2 * bin(engines(a, b)).count("1")

    def send(dsts, sem, codes, plane):
        ids = [DstId(rid=topo.addr(cores[d[0]])[0], pnc=topo.addr(cores[d[0]])[1]) for d in dsts]
        mask = engines(rank, dsts[0][0])
        for src, lands in ((codes.bitcast(dt.uint8), [d[1].bitcast(dt.uint8) for d in dsts]), (plane, [d[2] for d in dsts])):
            g.remote_dma_fused([RemoteDMATransfer(dst_ids=ids, dma_engine_mask=mask, remote_sem=T.sem[sem], srcs=[src], dsts=lands)],
                               local_sem=T.sem.sent)
            count["sent"] += bin(mask).count("1")

    did("ldb", g.sync.dma_start(T.bt[:, :], T.b[:, :]), 16)
    did("lda0", g.sync.dma_start(T.at[:, 0:1024], T.a[:, 0:1024]), 16)
    did("lda1", g.sync.dma_start(T.at[:, 1024:2048], T.a[:, 1024:2048]), 16)

    lo, hi = (0, 512 - SHARE) if lower else (SHARE, 512)
    first = 0 if lower else 3
    mine, theirs = ((0, SHARE), (512 - SHARE, 512)) if lower else ((512 - SHARE, 512), (0, SHARE))
    rest = (128, hi) if lower else (lo, 384)
    ones = did("v", g.vector.memset(T.ones[:, :], 1.0))
    zero = [did("v", g.vector.memset(T.sel[:, 512 * first:512 * first + 512], 0.0))]
    zero.append(did("v", g.vector.memset(T.sel[:, 4 * rest[0]:4 * rest[1]], 0.0)))
    need("g", "v", ones)
    made = did("gs", g.affine_select(T.diag[:, :], T.ones[:, :], [[-1, 128]], AluOpType.is_equal, 0.0, 0, 1))
    need("s", "gs", made)
    placed = []
    for b in [first] + [b for b in range(4) if b != first]:
        need("s", "v", zero[b != first])
        a, z = max(lo, 128 * b), min(hi, 128 * b + 128)
        placed.append(did("s", g.scalar.activation(T.sel[:, 4 * a + b:4 * z:4], T.diag[:, a - 128 * b:z - 128 * b],
                                                   ActivationFunctionType.Copy)))
    need("v", "s", placed[0])
    share = did("v", g.vector.quantize_mx(words("qsel", first), words("ssel", first), T.sel[:, 512 * first:512 * first + 512]))
    need("g", "v", share)
    codes, plane = T.qsel[:, mine[0]:mine[1]], T.ssel[:, mine[0]:mine[1]]
    send([(partner, codes, plane)], "arrsel", codes, plane)

    need("v", "ldb", 16)
    did("v", g.vector.quantize_mx(T.qb[:, :], T.sb[:, :], T.bt[:, :]))
    ready = []
    for i in range(4):
        need("v", "lda%d" % (i // 2), 16)
        ready.append(did("v", g.vector.quantize_mx(words("qa", i), words("sa", i), T.at[:, 512 * i:512 * i + 512])))

    bank = [0] * 4
    state = {"set": 1, "readers": [{}, {}]}

    def region(i):
        c = 2048 * state["set"] + 512 * i
        return T.ps[:, c:c + 128]

    def build(tiles):
        state["set"] = 1 - state["set"]
        readers = state["readers"][state["set"]]
        for q in readers:
            need("t", q, readers[q])
        for i in range(4):
            need("t", "v", ready[i])
            for k in range(2):
                call = g.tensor.matmul_mx(region(i), words("qa", i), words("sa", i), words("qb", k), words("sb", k),
                                          k == 0, k == 1 and not tiles)
            bank[i] = did("t", call)
        for m in tiles:
            k = slot[m]
            need("t", "v", selected[0])
            need("t", "arrsel", arrivals(partner, rank))
            need("t", "arr%d" % k, arrivals(m[0], rank))
            for b in range(4):
                bank[b] = did("t", g.tensor.matmul_mx(region(b), words("qsel", b), words("ssel", b), T["ql%d" % k][:, :],
                                                      T["sl%d" % k][:, :], False, m == tiles[-1]))

    def copy_out(name, by):
        last = state["readers"][state["set"]]
        for i in range(4):
            q = by[i]
            need(q, "t", bank[i])
            view = T[name][:, i:512:4]
            if q == "s":
                last[q] = did(q, g.scalar.activation(view, region(i), ActivationFunctionType.Copy))
            else:
                last[q] = did(q, g.vector.tensor_copy(view, region(i)))
        return last

    def pack(name, codes, plane, by):
        last = copy_out(name, by)
        for q in last:
            need("v", q, last[q])
        packed = did("v", g.vector.quantize_mx(T[codes][:, :], T[plane][:, :], T[name][:, :]))
        need("g", "v", packed)

    def store(by):
        last = copy_out("yt", by)
        for q in last:
            need("y", q, last[q])
        did("st", g.sync.dma_start(T.y[:, :], T.yt[:, :]), 16)

    def post(group, codes, plane):
        send([(m[1], T["ql%d" % slot[m]][:, :], T["sl%d" % slot[m]][:, :]) for m in group], "arr%d" % slot[group[0]],
             T[codes][:, :], T[plane][:, :])

    P_BY, Y_BY = "sssv", "svsv"
    if sends_p or not addends:
        build([])
        if sends_p:
            pack("hp", "qp", "sp", P_BY)
            for m in sorted([m for m in outbox if m[2] == "P"], key=hops):
                post([m], "qp", "sp")
        if not addends:
            store(P_BY)
    need("v", "s", placed[-1])
    selected = [did("v", g.vector.quantize_mx(T.qsel[:, rest[0]:rest[1]], T.ssel[:, rest[0]:rest[1]],
                                              T.sel[:, 4 * rest[0]:4 * rest[1]]))]

    if forwards:
        k = slot[from_partner[0]]
        need("g", "arr%d" % k, arrivals(partner, rank))
        post(forwards, "ql%d" % k, "sl%d" % k)
    if sends_s:
        build(from_partner)
        pack("hs", "qs", "ss", Y_BY)
        for m in [m for m in outbox if m[2] == "S"]:
            post([m], "qs", "ss")

    if addends:
        build(addends)
        store(Y_BY)

    for sem in ("v", "s", "t", "gs", "st"):
        need("y", sem, count[sem])
    need("g", "sent", count["sent"])
